import numpy as np
import ml_dtypes


def mxq(x, axis, fmt="e4m3"):
    dtype, down = {"e4m3": (ml_dtypes.float8_e4m3fn, 7), "e5m2": (ml_dtypes.float8_e5m2, 14)}[fmt]
    v = np.moveaxis(np.asarray(x, np.float32).astype(ml_dtypes.bfloat16).astype(np.float64), axis, -1)
    blocks = v.reshape(v.shape[:-1] + (-1, 32))
    amax = np.abs(blocks).max(-1, keepdims=True)
    byte = np.maximum(np.where(amax > 0, np.frexp(amax)[1] - 1 + 127, 0) - down, 1)
    scale = np.exp2(byte - 127.0)
    codes = (blocks / scale).astype(np.float32).astype(dtype).astype(np.float64)
    return np.moveaxis((codes * scale).reshape(v.shape), -1, axis)


WIDE = False


def mx_kscale(k):
    if not WIDE:
        return np.ones(k)
    levels = np.array([10, -10, 5, -5, 0])
    if k % 512:
        return np.exp2(np.random.permutation(np.resize(levels, k // 32))).repeat(32)
    a = np.empty((k // 512, 16))
    for p in range(k // 512):
        a[p, :8] = np.random.permutation(np.resize(levels, 8))
        for g in range(8):
            far = levels[np.abs(levels - a[p, g]) >= 10]
            a[p, g + 8] = far[np.random.randint(len(far))]
    return np.exp2(a.ravel()).repeat(32)


def f64(x):
    return np.asarray(x).astype(np.float64)


def striped(idx):
    return np.tile(idx.reshape(-1, 16).T, (8, 1)).astype(np.uint16)


def unstriped(offs):
    return offs[:16].T.reshape(-1).astype(np.int64)


E2M1 = np.array([0.0, 0.5, 1.0, 1.5, 2.0, 3.0, 4.0, 6.0, -0.0, -0.5, -1.0, -1.5, -2.0, -3.0, -4.0, -6.0])


def pack_weight(w, fmt):
    k, n = w.shape
    w = f64(np.asarray(w, np.float32).astype(ml_dtypes.bfloat16)).reshape(k // 32, 32, n)
    amax = np.abs(w).max(1)
    if fmt == "e4m3":
        byte = np.frexp(amax)[1] - 1 + 127 - 7
    else:
        mant, ex = np.frexp(amax / 6.0)
        byte = np.where(mant > 0.5, ex, ex - 1) + 127
    byte = np.clip(np.where(amax > 0, byte, 1), 1, 254)
    scaled = (w * np.exp2(127.0 - byte)[:, None, :]).reshape(k, n).astype(np.float32)
    by_word = np.ascontiguousarray(scaled.reshape(k // 512, 128, 4, n).transpose(0, 1, 3, 2))
    if fmt == "e4m3":
        words = by_word.astype(ml_dtypes.float8_e4m3fn).view(np.uint8)
    else:
        c = by_word.astype(ml_dtypes.float4_e2m1fn).view(np.uint8) & 0xF
        words = (c[..., 0::2] | (c[..., 1::2] << 4)).reshape(k // 512, 128, 2 * n)
    return np.ascontiguousarray(words), np.ascontiguousarray(byte.astype(np.uint8).reshape(k // 512, 16, n))


def unpack_weight(words, scales, fmt):
    g, _, n = scales.shape
    words = np.ascontiguousarray(words).reshape(g, 128, n, -1)
    if fmt == "e4m3":
        vals = words.view(ml_dtypes.float8_e4m3fn).astype(np.float64)
    else:
        nib = np.empty((g, 128, n, 4), np.uint8)
        nib[..., 0::2] = words & 0xF
        nib[..., 1::2] = words >> 4
        vals = E2M1[nib]
    vals = vals * np.repeat(np.exp2(scales.astype(np.float64) - 127.0), 8, axis=1)[..., None]
    return vals.transpose(0, 1, 3, 2).reshape(g * 512, n)


def planes(y):
    n, m = y.shape
    v = y.astype(np.float32).astype(ml_dtypes.bfloat16).astype(np.float64).reshape(n // 32, 32, m)
    top = np.abs(v).max(1)
    byte = np.clip(np.where(top > 0, np.frexp(top)[1] - 1 + 127 - 7, 1), 1, 254)
    codes = (v * np.exp2(127.0 - byte)[:, None, :]).reshape(n, m).astype(np.float32).astype(ml_dtypes.float8_e4m3fn).view(np.uint8)
    words = codes.reshape(n // 512, 128, 4, m).transpose(0, 1, 3, 2)
    return np.ascontiguousarray(words), np.ascontiguousarray(byte.astype(np.uint8).reshape(n // 512, 16, m))


def relu(v):
    return np.maximum(v, 0.0)


K, T, E, C, H, N, TOP = 1024, 512, 12, 128, 512, 512, 3


def by_expert(wq, xq):
    return np.concatenate([wq[e].T @ xq[:, e * C:(e + 1) * C] for e in range(E)], axis=1)


def setup_inputs():
    n = np.random.standard_normal
    s = mx_kscale(K)
    u = mx_kscale(H)
    deal = np.repeat(np.arange(E), C).reshape(TOP, T)[:, np.random.permutation(T)]
    deal = np.take_along_axis(deal, np.argsort(np.random.rand(TOP, T), axis=0), axis=0)
    for _ in range(8):
        s_, t_ = np.random.permutation(T).reshape(2, -1); r = np.random.randint(TOP, size=T // 2); x, y = deal[r, s_].copy(), deal[r, t_].copy()
        ok = ~((deal[:, s_] == y).any(0) | (deal[:, t_] == x).any(0)); deal[r[ok], s_[ok]] = y[ok]; deal[r[ok], t_[ok]] = x[ok]
    order = np.lexsort((np.random.rand(TOP * T), deal.reshape(-1)))
    slot_token = order % T; pos = np.empty(TOP * T, np.int64); pos[order] = np.arange(TOP * T); pos = pos.reshape(TOP, T)
    g = np.random.uniform(0.5, 1.5, (TOP, T)); g = g / g.sum(0)
    x = pack_weight(n((K, T)) * s[:, None], "e4m3")
    w2 = [pack_weight(m, "e2m1") for m in n((E, H, N)) / np.sqrt(H) / u[None, :, None]]
    return {
        "x_words": x[0],
        "x_scales": x[1],
        "w1": (n((K, H)) / np.sqrt(K) / s[:, None] * u).astype(np.float32),
        "w2_words": np.stack([m[0] for m in w2]),
        "w2_scales": np.stack([m[1] for m in w2]),
        "gate": np.stack([np.tile(r, (128, 1)) for r in g]).astype(np.float32),
        "offs": striped(slot_token),
        "pos1": striped(pos[0]),
        "pos2": striped(pos[1]),
        "pos3": striped(pos[2]),
    }


def reference(x_words, x_scales, w1, w2_words, w2_scales, gate, offs, pos1, pos2, pos3):
    w1q = mxq(f64(w1), 0, "e4m3")
    w2 = np.stack([unpack_weight(w2_words[e], w2_scales[e], "e2m1") for e in range(E)])
    idx = unstriped(offs)
    x = unpack_weight(x_words, x_scales, "e4m3")
    h = relu(w1q.T @ x)
    y = by_expert(w2, mxq(h[:, idx], 0, "e4m3"))
    out = sum(f64(gate[r, :1]) * y[:, unstriped(p)] for r, p in enumerate((pos1, pos2, pos3)))
    out_0 = out
    return (out_0,) + planes(out_0)

@@ -1,0 +1,331 @@
+from contextlib import ExitStack
+
+import concourse.mybir as mybir
+from concourse.masks import make_identity
+
+K, T, E, C, H, N, TOP = 1024, 512, 12, 128, 512, 512, 3
+SLOTS = E * C
+FLOPS = 2 * K * H * T + 2 * H * N * SLOTS
+
+F32 = mybir.dt.float32
+BF16 = mybir.dt.bfloat16
+I32 = mybir.dt.int32
+U32 = mybir.dt.uint32
+U16 = mybir.dt.uint16
+U8 = mybir.dt.uint8
+FP8X4 = mybir.dt.float8_e4m3fn_x4
+FP4X4 = mybir.dt.float4_e2m1fn_x4
+ACT = mybir.ActivationFunctionType
+MULT = mybir.AluOpType.mult
+
+P = 128
+PACK = 4
+PASSES = K // (P * PACK)
+GROUP = 3
+GROUPS = E // GROUP
+GSLOTS = GROUP * C
+HALF = T // 2
+V_SHARE = 44
+
+
+def tile_moe_sup_lin_relu_kernel(
+    tc, x_words, x_scales, w1, w2_words, w2_scales, gate, offs, pos1, pos2, pos3, out_0, out_1, out_2
+):
+    nc = tc.nc
+    with ExitStack() as ctx:
+        keep = ctx.enter_context(tc.tile_pool(name="keep", bufs=1))
+        psum = ctx.enter_context(tc.psum_pool(name="psum", bufs=1))
+        banks = [psum.tile([P, 512], F32, name="bank%d" % i) for i in range(8)]
+
+        x_plane = keep.tile([P, PASSES, T], U8, name="x_plane", align_bytes=64)
+        w2_plane = keep.tile([P, E, N], U8, name="w2_plane", align_bytes=64)
+        nc.vector.memset(x_plane[:].rearrange("p s t -> p (s t)").bitcast(I32), 0)
+        nc.vector.memset(w2_plane[:].rearrange("p e n -> p (e n)").bitcast(I32), 0)
+        ident = keep.tile([P, P], F32, name="ident")
+        make_identity(nc, ident[:])
+
+        w1_rows = w1.rearrange("(s p j) c -> s p j c", s=PASSES, j=PACK)
+        w1_first = keep.tile([P, PACK, H], F32, name="w1_first")
+        nc.sync.dma_start(out=w1_first[:], in_=w1_rows[0])
+        for r in range(4):
+            nc.sync.dma_start(
+                out=x_plane[r:P:32, :, :].bitcast(I32),
+                in_=x_scales[:, r:16:4, :].rearrange("s q t -> q s t").bitcast(I32),
+            )
+        x_codes = [keep.tile([P, T], U32, name="x_codes%d" % s, align_bytes=64) for s in range(PASSES)]
+
+        def load_x(s):
+            nc.sync.dma_start(
+                out=x_codes[s][:].bitcast(I32), in_=x_words[s].rearrange("p t d -> p (t d)").bitcast(I32)
+            )
+
+        load_x(0)
+        w1_second = [keep.tile([P, PACK, H // 2], F32, name="w1_second%d" % a) for a in range(2)]
+        for a in range(2):
+            nc.sync.dma_start(out=w1_second[a][:], in_=w1_rows[1][:, :, a * (H // 2) : (a + 1) * (H // 2)])
+        load_x(1)
+        offs_t = keep.tile([P, SLOTS // 16], U16, name="offs_t")
+        nc.sync.dma_start(offs_t[:], offs)
+        for r in range(4):
+            nc.sync.dma_start(
+                out=w2_plane[r:P:32, :, :].bitcast(I32),
+                in_=w2_scales[:, 0, r:16:4, :].rearrange("e q n -> q e n").bitcast(I32),
+            )
+        w2_codes = [keep.tile([P, GROUP, 2 * N], U8, name="w2_codes%d" % g, align_bytes=64) for g in range(GROUPS)]
+        for g in range(GROUPS):
+            nc.sync.dma_start(
+                out=w2_codes[g][:].bitcast(I32),
+                in_=w2_words[GROUP * g : GROUP * (g + 1), 0].rearrange("e p b -> p e b").bitcast(I32),
+            )
+        pos_t = [keep.tile([P, T // 16], U16, name="pos_t%d" % r) for r in range(TOP)]
+        for r, pos in enumerate((pos1, pos2, pos3)):
+            nc.sync.dma_start(pos_t[r][:], pos)
+        gate_rows = keep.tile([P, TOP - 1, T], F32, name="gate_rows")
+        nc.sync.dma_start(out=gate_rows[:], in_=gate[: TOP - 1].rearrange("r p t -> p r t"))
+        assisted = 0 * P
+        gate_last = keep.tile([P, T - assisted], F32, name="gate_last")
+        nc.sync.dma_start(out=gate_last[:], in_=gate[TOP - 1, :, assisted:])
+
+        w1_bf = [keep.tile([P, PACK, P, PACK], BF16, name="w1_bf%d" % s, align_bytes=64) for s in range(PASSES)]
+        w1_codes = [keep.tile([P, H], U32, name="w1_codes%d" % s, align_bytes=64) for s in range(PASSES)]
+        w1_plane = [keep.tile([P, H], U8, name="w1_plane%d" % s, align_bytes=64) for s in range(PASSES)]
+
+        def round_w1(on_scalar, s, raw, raw_m0, m0, m1):
+            src = raw[:].rearrange("p j (m d) -> p m d j", d=PACK)[:, m0 - raw_m0 : m1 - raw_m0]
+            dst = w1_bf[s][:].rearrange("p d m j -> p m d j")[:, m0:m1]
+            if on_scalar:
+                nc.scalar.activation(dst, src, ACT.Copy)
+            else:
+                nc.vector.tensor_copy(out=dst, in_=src)
+
+        def quantize_w1(s, u):
+            cols = slice(2 * P * u, 2 * P * (u + 1))
+            nc.vector.quantize_mx(
+                out=w1_codes[s][:, cols].bitcast(FP8X4),
+                scales=w1_plane[s][:, cols],
+                in_=w1_bf[s][:, 2 * u : 2 * u + 2].rearrange("p d m j -> p (d m j)"),
+            )
+
+        round_w1(False, 0, w1_first, 0, 0, 64)
+        round_w1(True, 0, w1_first, 0, 64, 128)
+        quantize_w1(0, 0)
+        quantize_w1(0, 1)
+        round_w1(False, 1, w1_second[0], 0, 0, 64)
+        round_w1(False, 1, w1_second[1], 64, 64, 64 + V_SHARE)
+        round_w1(True, 1, w1_second[1], 64, 64 + V_SHARE, 128)
+        quantize_w1(1, 0)
+        quantize_w1(1, 1)
+
+        h_acc = [[banks[2 * u + th][:].rearrange("p (e t) -> p e t", e=2) for th in range(2)] for u in range(2)]
+        for s in range(PASSES):
+            for u in range(2):
+                for th in range(2):
+                    for e in range(2):
+                        d = 2 * u + e
+                        nc.tensor.matmul_mx(
+                            out=h_acc[u][th][:, e, :],
+                            lhsT=w1_codes[s][:, P * d : P * (d + 1)].bitcast(FP8X4),
+                            lhsT_scale=w1_plane[s][:, P * d : P * (d + 1)],
+                            rhs=x_codes[s][:, HALF * th : HALF * (th + 1)].bitcast(FP8X4),
+                            rhs_scale=x_plane[:, s, HALF * th : HALF * (th + 1)],
+                            start=(s == 0 and e == 0),
+                            stop=(s == PASSES - 1 and e == 1),
+                        )
+        h_pairs = keep.tile([P, 2 * T], U32, name="h_pairs")
+        for u in range(2):
+            for th in range(2):
+                dst = h_pairs[:, T * u + HALF * th : T * u + HALF * (th + 1)].bitcast(BF16).rearrange("p (t e) -> p t e", e=2)
+                src = h_acc[u][th].rearrange("p e t -> p t e")
+                if u == 0 and th == 1:
+                    nc.vector.tensor_scalar_max(dst, src, 0.0)
+                else:
+                    nc.scalar.activation(dst, src, ACT.Relu)
+
+        slot_codes = [keep.tile([P, GSLOTS], U32, name="slot_codes%d" % g, align_bytes=64) for g in range(GROUPS)]
+        slot_plane = [keep.tile([P, GSLOTS], U8, name="slot_plane%d" % g, align_bytes=64) for g in range(GROUPS)]
+        y_rows = [keep.tile([P, SLOTS], F32, name="y_rows%d" % j) for j in range(PACK)]
+        stage = [keep.tile([P, 2 * GSLOTS], U32, name="stage%d" % i, align_bytes=64) for i in range(3)]
+
+        def pick(g, u):
+            cols = slice(g * GSLOTS // 16, (g + 1) * GSLOTS // 16)
+            window = h_pairs[:] if (g > 0 and u == 0) else h_pairs[:, T * u : T * (u + 1)]
+            dst = stage[2 * g % 3][:, GSLOTS * u : GSLOTS * (u + 1)]
+            nc.vector.tensor_copy(out=dst, in_=window.indirect(offs_t[:, cols]))
+
+        def weave_and_quantize(g):
+            picked, woven = stage[2 * g % 3], stage[(2 * g + 1) % 3]
+            if g == GROUPS - 1:
+                nc.vector.tensor_copy(
+                    out=woven[:].bitcast(I32).rearrange("p (s u) -> p s u", u=2),
+                    in_=picked[:].bitcast(I32).rearrange("p (u s) -> p s u", u=2),
+                )
+            else:
+                nc.scalar.copy(
+                    out=woven[:].rearrange("p (s u) -> p s u", u=2), in_=picked[:].rearrange("p (u s) -> p s u", u=2)
+                )
+            nc.vector.quantize_mx(
+                out=slot_codes[g][:].bitcast(FP8X4),
+                scales=slot_plane[g][:],
+                in_=woven[:].bitcast(BF16),
+            )
+
+        y_used = []
+
+        def experts(g, j, on_vector=False):
+            y_acc = banks[(4 + len(y_used)) % 8]
+            y_used.append((g, j))
+            for i in range(GROUP):
+                cols = slice(C * i, C * (i + 1))
+                nc.tensor.matmul_mx(
+                    out=y_acc[:, cols],
+                    lhsT=w2_codes[g][:, i, 2 * P * j : 2 * P * (j + 1)].bitcast(FP4X4),
+                    lhsT_scale=w2_plane[:, GROUP * g + i, P * j : P * (j + 1)],
+                    rhs=slot_codes[g][:, cols].bitcast(FP8X4),
+                    rhs_scale=slot_plane[g][:, cols],
+                    start=True,
+                    stop=True,
+                )
+            dst = y_rows[j][:, GSLOTS * g : GSLOTS * (g + 1)]
+            if on_vector:
+                nc.vector.tensor_copy(out=dst, in_=y_acc[:, :GSLOTS])
+            else:
+                nc.scalar.copy(out=dst, in_=y_acc[:, :GSLOTS])
+
+        pick(0, 0)
+        pick(0, 1)
+        weave_and_quantize(0)
+        pick(1, 0)
+        pick(1, 1)
+        weave_and_quantize(1)
+        pick(2, 0)
+        pick(2, 1)
+        for j in range(3):
+            experts(0, j)
+        weave_and_quantize(2)
+        pick(3, 0)
+        pick(3, 1)
+        weave_and_quantize(3)
+        experts(0, 3)
+        for j in range(PACK):
+            experts(1, j)
+        for j in range(3):
+            experts(2, j)
+        experts(2, 3, True)
+        experts(3, 0, True)
+        for j in range(1, PACK):
+            experts(3, j)
+
+        out_rows = out_0.rearrange("(m d) t -> m d t", d=PACK)
+        out_words = out_1[0].rearrange("p t d -> p (t d)").bitcast(I32)
+        out_plane = keep.tile([P, T], U8, name="out_plane", align_bytes=64)
+        prods = [keep.tile([P, HALF], F32, name="prod%d" % i) for i in range(4)]
+        plains = []
+        prods_made = []
+
+        def turn(bank, j, src, b, start, stop):
+            nc.tensor.matmul(
+                bank[:, P * j : P * (j + 1)], src[:, P * b : P * (b + 1)], ident[:],
+                start=start, stop=stop, is_transpose=True,
+            )
+
+        def fetch_plain(t0, width, j):
+            cols = slice(t0 // 16, (t0 + width) // 16)
+            nc.scalar.activation(plains[j][:, t0 : t0 + width], y_rows[j][:].indirect(pos_t[TOP - 1][:, cols]), ACT.Copy)
+
+        def turn_plain(b, bank):
+            for j in range(PACK):
+                turn(bank, j, plains[j], b, True, True)
+
+        def fetch(t0, width, j, sum_banks):
+            cols = slice(t0 // 16, (t0 + width) // 16)
+            fused = TOP - 1 if t0 < assisted else TOP
+            for r in range(fused):
+                prod = prods[len(prods_made) % len(prods)]
+                prods_made.append(r)
+                weights = gate_rows[:, r, t0 : t0 + width] if r < TOP - 1 else gate_last[:, t0 - assisted : t0 - assisted + width]
+                nc.vector.tensor_tensor(prod[:, :width], y_rows[j][:].indirect(pos_t[r][:, cols]), weights, MULT)
+                for b, bank in enumerate(sum_banks):
+                    turn(bank, j, prod, b, r == 0, r == fused - 1)
+
+        dealt = [keep.tile([P, PACK, P], F32, name="dealt%d" % b) for b in range(4)]
+        dealt_lone = [keep.tile([P, PACK, P], F32, name="dealt_lone%d" % b) for b in range(assisted // P)]
+        out_f32 = keep.tile([P, PACK, T], F32, name="out_f32")
+        out_bf = keep.tile([P, T, PACK], BF16, name="out_bf", align_bytes=64)
+        out_codes = keep.tile([P, T], U32, name="out_codes", align_bytes=64)
+
+        def deal(b, bank, j0, j1, on_vector=False):
+            src = bank[:, P * j0 : P * j1].rearrange("p (m d) -> p d m", d=PACK)
+            dst = dealt[b][:, :, 32 * j0 : 32 * j1]
+            if on_vector:
+                nc.vector.tensor_copy(out=dst, in_=src)
+            else:
+                nc.scalar.copy(out=dst, in_=src)
+
+
+        def turn_back(b, bank):
+            parts = [dealt[b]] + ([dealt_lone[b]] if b < assisted // P else [])
+            for d in range(PACK):
+                for i, part in enumerate(parts):
+                    nc.tensor.matmul(
+                        bank[:, P * d : P * (d + 1)], part[:, d, :], ident[:],
+                        start=(i == 0), stop=(i == len(parts) - 1), is_transpose=True,
+                    )
+
+        def leave_f32(b, bank):
+            nc.scalar.copy(out=out_f32[:, :, P * b : P * (b + 1)], in_=bank[:].rearrange("p (d t) -> p d t", d=PACK))
+
+        def round_sbuf(t0, t1):
+            nc.vector.tensor_copy(out=out_bf[:, t0:t1, :], in_=out_f32[:, :, t0:t1].rearrange("p d t -> p t d"))
+
+        def round_out(b, bank, on_vector=False):
+            src = bank[:].rearrange("p (d t) -> p t d", d=PACK)
+            dst = out_bf[:, P * b : P * (b + 1), :]
+            if on_vector:
+                nc.vector.tensor_copy(out=dst, in_=src)
+            else:
+                nc.scalar.copy(out=dst, in_=src)
+
+        def store_f32(t0, t1):
+            nc.sync.dma_start(out=out_rows[:, :, t0:t1], in_=out_f32[:, :, t0:t1])
+
+        def quantize_out(t0, t1):
+            nc.vector.quantize_mx(
+                out=out_codes[:, t0:t1].bitcast(FP8X4),
+                scales=out_plane[:, t0:t1],
+                in_=out_bf[:, t0:t1, :].rearrange("p t d -> p (t d)"),
+            )
+            nc.sync.dma_start(out=out_words[:, t0:t1], in_=out_codes[:, t0:t1].bitcast(I32))
+
+        def leave(b, bank):
+            leave_f32(b, bank)
+            round_out(b, bank)
+
+        for j in range(PACK):
+            fetch(0, 2 * P, j, banks[4:6])
+        for b in range(2):
+            deal(b, banks[4 + b], 0, PACK)
+            turn_back(b, banks[b])
+        for j in range(PACK):
+            fetch(2 * P, P, j, banks[6:7])
+        for b in range(2):
+            leave(b, banks[b])
+        store_f32(0, 2 * P)
+        quantize_out(0, 2 * P)
+        deal(2, banks[6], 0, PACK)
+        turn_back(2, banks[2])
+        for j in range(PACK - 1):
+            fetch(3 * P, P, j, banks[7:8])
+        leave(2, banks[2])
+        store_f32(2 * P, 3 * P)
+        quantize_out(2 * P, 3 * P)
+        deal(3, banks[7], 0, PACK - 1)
+        fetch(3 * P, P, PACK - 1, banks[4:5])
+        deal(3, banks[4], PACK - 1, PACK)
+        turn_back(3, banks[3])
+        leave_f32(3, banks[3])
+        store_f32(3 * P, 4 * P)
+        round_sbuf(3 * P, 4 * P)
+        quantize_out(3 * P, 4 * P)
+
+        for r in range(4):
+            nc.sync.dma_start(out=out_2[0, r:16:4, :].bitcast(I32), in_=out_plane[r:P:32, :].bitcast(I32))

@@ -21,21 +21,28 @@ MULT = mybir.AluOpType.mult
 P = 128
 PACK = 4
 PASSES = K // (P * PACK)
-GROUP = 3
-GROUPS = E // GROUP
-GSLOTS = GROUP * C
+GROUPS = (3, 3, 3, 3)
 HALF = T // 2
 V_SHARE = 44
+RING = 6
 
 
 def tile_moe_sup_lin_relu_kernel(
     tc, x_words, x_scales, w1, w2_words, w2_scales, gate, offs, pos1, pos2, pos3, out_0, out_1, out_2
 ):
     nc = tc.nc
+    first_expert = [sum(GROUPS[:g]) for g in range(len(GROUPS) + 1)]
+    last = len(GROUPS) - 1
     with ExitStack() as ctx:
         keep = ctx.enter_context(tc.tile_pool(name="keep", bufs=1))
         psum = ctx.enter_context(tc.psum_pool(name="psum", bufs=1))
         banks = [psum.tile([P, 512], F32, name="bank%d" % i) for i in range(8)]
+
+        def move(on_vector, dst, src):
+            if on_vector:
+                nc.vector.tensor_copy(out=dst, in_=src)
+            else:
+                nc.scalar.copy(out=dst, in_=src)
 
         x_plane = keep.tile([P, PASSES, T], U8, name="x_plane", align_bytes=64)
         w2_plane = keep.tile([P, E, N], U8, name="w2_plane", align_bytes=64)
@@ -71,32 +78,31 @@ def tile_moe_sup_lin_relu_kernel(
                 out=w2_plane[r:P:32, :, :].bitcast(I32),
                 in_=w2_scales[:, 0, r:16:4, :].rearrange("e q n -> q e n").bitcast(I32),
             )
-        w2_codes = [keep.tile([P, GROUP, 2 * N], U8, name="w2_codes%d" % g, align_bytes=64) for g in range(GROUPS)]
-        for g in range(GROUPS):
+        w2_codes = [
+            keep.tile([P, size, 2 * N], U8, name="w2_codes%d" % g, align_bytes=64) for g, size in enumerate(GROUPS)
+        ]
+        for g in range(len(GROUPS)):
             nc.sync.dma_start(
                 out=w2_codes[g][:].bitcast(I32),
-                in_=w2_words[GROUP * g : GROUP * (g + 1), 0].rearrange("e p b -> p e b").bitcast(I32),
+                in_=w2_words[first_expert[g] : first_expert[g + 1], 0].rearrange("e p b -> p e b").bitcast(I32),
             )
         pos_t = [keep.tile([P, T // 16], U16, name="pos_t%d" % r) for r in range(TOP)]
         for r, pos in enumerate((pos1, pos2, pos3)):
             nc.sync.dma_start(pos_t[r][:], pos)
-        gate_rows = keep.tile([P, TOP - 1, T], F32, name="gate_rows")
-        nc.sync.dma_start(out=gate_rows[:], in_=gate[: TOP - 1].rearrange("r p t -> p r t"))
-        assisted = 0 * P
-        gate_last = keep.tile([P, T - assisted], F32, name="gate_last")
-        nc.sync.dma_start(out=gate_last[:], in_=gate[TOP - 1, :, assisted:])
+        gate_t = keep.tile([P, TOP, T], F32, name="gate_t")
+        nc.sync.dma_start(out=gate_t[:], in_=gate.rearrange("r p t -> p r t"))
 
         w1_bf = [keep.tile([P, PACK, P, PACK], BF16, name="w1_bf%d" % s, align_bytes=64) for s in range(PASSES)]
         w1_codes = [keep.tile([P, H], U32, name="w1_codes%d" % s, align_bytes=64) for s in range(PASSES)]
         w1_plane = [keep.tile([P, H], U8, name="w1_plane%d" % s, align_bytes=64) for s in range(PASSES)]
 
-        def round_w1(on_scalar, s, raw, raw_m0, m0, m1):
+        def round_w1(on_vector, s, raw, raw_m0, m0, m1):
             src = raw[:].rearrange("p j (m d) -> p m d j", d=PACK)[:, m0 - raw_m0 : m1 - raw_m0]
             dst = w1_bf[s][:].rearrange("p d m j -> p m d j")[:, m0:m1]
-            if on_scalar:
-                nc.scalar.activation(dst, src, ACT.Copy)
-            else:
+            if on_vector:
                 nc.vector.tensor_copy(out=dst, in_=src)
+            else:
+                nc.scalar.activation(dst, src, ACT.Copy)
 
         def quantize_w1(s, u):
             cols = slice(2 * P * u, 2 * P * (u + 1))
@@ -106,13 +112,13 @@ def tile_moe_sup_lin_relu_kernel(
                 in_=w1_bf[s][:, 2 * u : 2 * u + 2].rearrange("p d m j -> p (d m j)"),
             )
 
-        round_w1(False, 0, w1_first, 0, 0, 64)
-        round_w1(True, 0, w1_first, 0, 64, 128)
+        round_w1(True, 0, w1_first, 0, 0, 2 * V_SHARE)
+        round_w1(False, 0, w1_first, 0, 2 * V_SHARE, P)
         quantize_w1(0, 0)
         quantize_w1(0, 1)
-        round_w1(False, 1, w1_second[0], 0, 0, 64)
-        round_w1(False, 1, w1_second[1], 64, 64, 64 + V_SHARE)
-        round_w1(True, 1, w1_second[1], 64, 64 + V_SHARE, 128)
+        for a in range(2):
+            round_w1(True, 1, w1_second[a], 64 * a, 64 * a, 64 * a + V_SHARE)
+            round_w1(False, 1, w1_second[a], 64 * a, 64 * a + V_SHARE, 64 * (a + 1))
         quantize_w1(1, 0)
         quantize_w1(1, 1)
 
@@ -134,142 +140,134 @@ def tile_moe_sup_lin_relu_kernel(
         h_pairs = keep.tile([P, 2 * T], U32, name="h_pairs")
         for u in range(2):
             for th in range(2):
-                dst = h_pairs[:, T * u + HALF * th : T * u + HALF * (th + 1)].bitcast(BF16).rearrange("p (t e) -> p t e", e=2)
+                first = T * u + HALF * th
+                dst = h_pairs[:, first : first + HALF].bitcast(BF16).rearrange("p (t e) -> p t e", e=2)
                 src = h_acc[u][th].rearrange("p e t -> p t e")
                 if u == 0 and th == 1:
                     nc.vector.tensor_scalar_max(dst, src, 0.0)
                 else:
                     nc.scalar.activation(dst, src, ACT.Relu)
 
-        slot_codes = [keep.tile([P, GSLOTS], U32, name="slot_codes%d" % g, align_bytes=64) for g in range(GROUPS)]
-        slot_plane = [keep.tile([P, GSLOTS], U8, name="slot_plane%d" % g, align_bytes=64) for g in range(GROUPS)]
+        slot_codes = keep.tile([P, SLOTS], U32, name="slot_codes", align_bytes=64)
+        slot_plane = keep.tile([P, SLOTS], U8, name="slot_plane", align_bytes=64)
         y_rows = [keep.tile([P, SLOTS], F32, name="y_rows%d" % j) for j in range(PACK)]
-        stage = [keep.tile([P, 2 * GSLOTS], U32, name="stage%d" % i, align_bytes=64) for i in range(3)]
+        stage = [keep.tile([P, 2 * C * max(GROUPS)], U32, name="stage%d" % i, align_bytes=64) for i in range(3)]
 
-        def pick(g, u):
-            cols = slice(g * GSLOTS // 16, (g + 1) * GSLOTS // 16)
-            window = h_pairs[:] if (g > 0 and u == 0) else h_pairs[:, T * u : T * (u + 1)]
-            dst = stage[2 * g % 3][:, GSLOTS * u : GSLOTS * (u + 1)]
-            nc.vector.tensor_copy(out=dst, in_=window.indirect(offs_t[:, cols]))
+        def pick(g):
+            width = C * GROUPS[g]
+            cols = slice(C * first_expert[g] // 16, C * first_expert[g + 1] // 16)
+            for u in range(2):
+                window = h_pairs[:] if (g > 0 and u == 0) else h_pairs[:, T * u : T * (u + 1)]
+                dst = stage[2 * g % 3][:, width * u : width * (u + 1)]
+                nc.vector.tensor_copy(out=dst, in_=window.indirect(offs_t[:, cols]))
 
         def weave_and_quantize(g):
-            picked, woven = stage[2 * g % 3], stage[(2 * g + 1) % 3]
-            if g == GROUPS - 1:
+            width = C * GROUPS[g]
+            picked, woven = stage[2 * g % 3][:, : 2 * width], stage[(2 * g + 1) % 3][:, : 2 * width]
+            if g == last:
                 nc.vector.tensor_copy(
-                    out=woven[:].bitcast(I32).rearrange("p (s u) -> p s u", u=2),
-                    in_=picked[:].bitcast(I32).rearrange("p (u s) -> p s u", u=2),
+                    out=woven.bitcast(I32).rearrange("p (s u) -> p s u", u=2),
+                    in_=picked.bitcast(I32).rearrange("p (u s) -> p s u", u=2),
                 )
             else:
                 nc.scalar.copy(
-                    out=woven[:].rearrange("p (s u) -> p s u", u=2), in_=picked[:].rearrange("p (u s) -> p s u", u=2)
+                    out=woven.rearrange("p (s u) -> p s u", u=2), in_=picked.rearrange("p (u s) -> p s u", u=2)
                 )
+            slots = slice(C * first_expert[g], C * first_expert[g + 1])
             nc.vector.quantize_mx(
-                out=slot_codes[g][:].bitcast(FP8X4),
-                scales=slot_plane[g][:],
-                in_=woven[:].bitcast(BF16),
+                out=slot_codes[:, slots].bitcast(FP8X4), scales=slot_plane[:, slots], in_=woven.bitcast(BF16)
             )
 
-        y_used = []
+        y_made = []
 
         def experts(g, j, on_vector=False):
-            y_acc = banks[(4 + len(y_used)) % 8]
-            y_used.append((g, j))
-            for i in range(GROUP):
-                cols = slice(C * i, C * (i + 1))
+            y_acc = banks[(4 + len(y_made)) % 8]
+            y_made.append((g, j))
+            for i in range(GROUPS[g]):
+                e = first_expert[g] + i
                 nc.tensor.matmul_mx(
-                    out=y_acc[:, cols],
+                    out=y_acc[:, C * i : C * (i + 1)],
                     lhsT=w2_codes[g][:, i, 2 * P * j : 2 * P * (j + 1)].bitcast(FP4X4),
-                    lhsT_scale=w2_plane[:, GROUP * g + i, P * j : P * (j + 1)],
-                    rhs=slot_codes[g][:, cols].bitcast(FP8X4),
-                    rhs_scale=slot_plane[g][:, cols],
+                    lhsT_scale=w2_plane[:, e, P * j : P * (j + 1)],
+                    rhs=slot_codes[:, C * e : C * (e + 1)].bitcast(FP8X4),
+                    rhs_scale=slot_plane[:, C * e : C * (e + 1)],
                     start=True,
                     stop=True,
                 )
-            dst = y_rows[j][:, GSLOTS * g : GSLOTS * (g + 1)]
-            if on_vector:
-                nc.vector.tensor_copy(out=dst, in_=y_acc[:, :GSLOTS])
-            else:
-                nc.scalar.copy(out=dst, in_=y_acc[:, :GSLOTS])
+            move(on_vector, y_rows[j][:, C * first_expert[g] : C * first_expert[g + 1]], y_acc[:, : C * GROUPS[g]])
 
-        pick(0, 0)
-        pick(0, 1)
-        weave_and_quantize(0)
-        pick(1, 0)
-        pick(1, 1)
-        weave_and_quantize(1)
-        pick(2, 0)
-        pick(2, 1)
-        for j in range(3):
-            experts(0, j)
-        weave_and_quantize(2)
-        pick(3, 0)
-        pick(3, 1)
-        weave_and_quantize(3)
-        experts(0, 3)
+        for g in range(len(GROUPS)):
+            pick(g)
+            if 2 <= g < last:
+                for j in range(PACK - 1):
+                    experts(g - 2, j)
+            weave_and_quantize(g)
+            if 3 <= g < last:
+                experts(g - 3, PACK - 1)
+        if last >= 3:
+            experts(last - 3, PACK - 1)
         for j in range(PACK):
-            experts(1, j)
-        for j in range(3):
-            experts(2, j)
-        experts(2, 3, True)
-        experts(3, 0, True)
-        for j in range(1, PACK):
-            experts(3, j)
+            experts(last - 2, j)
+        for j in range(PACK):
+            experts(last - 1, j, j == PACK - 1)
+        for j in range(PACK):
+            experts(last, j, j == 0)
 
         out_rows = out_0.rearrange("(m d) t -> m d t", d=PACK)
         out_words = out_1[0].rearrange("p t d -> p (t d)").bitcast(I32)
         out_plane = keep.tile([P, T], U8, name="out_plane", align_bytes=64)
-        prods = [keep.tile([P, HALF], F32, name="prod%d" % i) for i in range(4)]
-        plains = []
+        prods = [keep.tile([P, HALF], F32, name="prod%d" % i) for i in range(RING)]
         prods_made = []
 
-        def turn(bank, j, src, b, start, stop):
-            nc.tensor.matmul(
-                bank[:, P * j : P * (j + 1)], src[:, P * b : P * (b + 1)], ident[:],
-                start=start, stop=stop, is_transpose=True,
-            )
+        def on_scalar(j, r):
+            return j > 0 and r > 0
 
-        def fetch_plain(t0, width, j):
+        plains = {
+            (j, r): keep.tile([P, T], F32, name="plain%d_%d" % (j, r))
+            for j in range(PACK)
+            for r in range(TOP)
+            if on_scalar(j, r)
+        }
+
+        def fetch_plain(t0, width):
             cols = slice(t0 // 16, (t0 + width) // 16)
-            nc.scalar.activation(plains[j][:, t0 : t0 + width], y_rows[j][:].indirect(pos_t[TOP - 1][:, cols]), ACT.Copy)
+            for j, r in plains:
+                nc.scalar.activation(
+                    plains[j, r][:, t0 : t0 + width], y_rows[j][:].indirect(pos_t[r][:, cols]), ACT.Copy
+                )
 
-        def turn_plain(b, bank):
-            for j in range(PACK):
-                turn(bank, j, plains[j], b, True, True)
-
-        def fetch(t0, width, j, sum_banks):
+        def weigh(t0, width, j, sum_banks):
             cols = slice(t0 // 16, (t0 + width) // 16)
-            fused = TOP - 1 if t0 < assisted else TOP
-            for r in range(fused):
-                prod = prods[len(prods_made) % len(prods)]
+            for r in range(TOP):
+                prod = prods[len(prods_made) % RING]
                 prods_made.append(r)
-                weights = gate_rows[:, r, t0 : t0 + width] if r < TOP - 1 else gate_last[:, t0 - assisted : t0 - assisted + width]
-                nc.vector.tensor_tensor(prod[:, :width], y_rows[j][:].indirect(pos_t[r][:, cols]), weights, MULT)
+                if on_scalar(j, r):
+                    values = plains[j, r][:, t0 : t0 + width]
+                else:
+                    values = y_rows[j][:].indirect(pos_t[r][:, cols])
+                nc.vector.tensor_tensor(prod[:, :width], values, gate_t[:, r, t0 : t0 + width], MULT)
                 for b, bank in enumerate(sum_banks):
-                    turn(bank, j, prod, b, r == 0, r == fused - 1)
+                    nc.tensor.matmul(
+                        bank[:, P * j : P * (j + 1)],
+                        prod[:, P * b : P * (b + 1)],
+                        ident[:],
+                        start=(r == 0),
+                        stop=(r == TOP - 1),
+                        is_transpose=True,
+                    )
 
         dealt = [keep.tile([P, PACK, P], F32, name="dealt%d" % b) for b in range(4)]
-        dealt_lone = [keep.tile([P, PACK, P], F32, name="dealt_lone%d" % b) for b in range(assisted // P)]
         out_f32 = keep.tile([P, PACK, T], F32, name="out_f32")
         out_bf = keep.tile([P, T, PACK], BF16, name="out_bf", align_bytes=64)
         out_codes = keep.tile([P, T], U32, name="out_codes", align_bytes=64)
 
         def deal(b, bank, j0, j1, on_vector=False):
             src = bank[:, P * j0 : P * j1].rearrange("p (m d) -> p d m", d=PACK)
-            dst = dealt[b][:, :, 32 * j0 : 32 * j1]
-            if on_vector:
-                nc.vector.tensor_copy(out=dst, in_=src)
-            else:
-                nc.scalar.copy(out=dst, in_=src)
-
+            move(on_vector, dealt[b][:, :, 32 * j0 : 32 * j1], src)
 
         def turn_back(b, bank):
-            parts = [dealt[b]] + ([dealt_lone[b]] if b < assisted // P else [])
             for d in range(PACK):
-                for i, part in enumerate(parts):
-                    nc.tensor.matmul(
-                        bank[:, P * d : P * (d + 1)], part[:, d, :], ident[:],
-                        start=(i == 0), stop=(i == len(parts) - 1), is_transpose=True,
-                    )
+                nc.tensor.transpose(bank[:, P * d : P * (d + 1)], dealt[b][:, d, :], ident[:])
 
         def leave_f32(b, bank):
             nc.scalar.copy(out=out_f32[:, :, P * b : P * (b + 1)], in_=bank[:].rearrange("p (d t) -> p d t", d=PACK))
@@ -278,15 +276,10 @@ def tile_moe_sup_lin_relu_kernel(
             nc.vector.tensor_copy(out=out_bf[:, t0:t1, :], in_=out_f32[:, :, t0:t1].rearrange("p d t -> p t d"))
 
         def round_out(b, bank, on_vector=False):
-            src = bank[:].rearrange("p (d t) -> p t d", d=PACK)
-            dst = out_bf[:, P * b : P * (b + 1), :]
-            if on_vector:
-                nc.vector.tensor_copy(out=dst, in_=src)
-            else:
-                nc.scalar.copy(out=dst, in_=src)
+            move(on_vector, out_bf[:, P * b : P * (b + 1), :], bank[:].rearrange("p (d t) -> p t d", d=PACK))
 
-        def store_f32(t0, t1):
-            nc.sync.dma_start(out=out_rows[:, :, t0:t1], in_=out_f32[:, :, t0:t1])
+        def store_f32(t0, t1, queue=nc.sync):
+            queue.dma_start(out=out_rows[:, :, t0:t1], in_=out_f32[:, :, t0:t1])
 
         def quantize_out(t0, t1):
             nc.vector.quantize_mx(
@@ -296,36 +289,40 @@ def tile_moe_sup_lin_relu_kernel(
             )
             nc.sync.dma_start(out=out_words[:, t0:t1], in_=out_codes[:, t0:t1].bitcast(I32))
 
-        def leave(b, bank):
-            leave_f32(b, bank)
-            round_out(b, bank)
+        def store_scales():
+            for r in range(4):
+                nc.sync.dma_start(out=out_2[0, r:16:4, :].bitcast(I32), in_=out_plane[r:P:32, :].bitcast(I32))
 
+        fetch_plain(0, 2 * P)
         for j in range(PACK):
-            fetch(0, 2 * P, j, banks[4:6])
+            weigh(0, 2 * P, j, banks[4:6])
+        fetch_plain(2 * P, P)
         for b in range(2):
             deal(b, banks[4 + b], 0, PACK)
             turn_back(b, banks[b])
         for j in range(PACK):
-            fetch(2 * P, P, j, banks[6:7])
+            weigh(2 * P, P, j, banks[6:7])
+        fetch_plain(3 * P, P)
         for b in range(2):
-            leave(b, banks[b])
+            leave_f32(b, banks[b])
         store_f32(0, 2 * P)
-        quantize_out(0, 2 * P)
         deal(2, banks[6], 0, PACK)
         turn_back(2, banks[2])
+        for b in range(2):
+            round_out(b, banks[b])
         for j in range(PACK - 1):
-            fetch(3 * P, P, j, banks[7:8])
-        leave(2, banks[2])
+            weigh(3 * P, P, j, banks[7:8])
+        leave_f32(2, banks[2])
         store_f32(2 * P, 3 * P)
-        quantize_out(2 * P, 3 * P)
         deal(3, banks[7], 0, PACK - 1)
-        fetch(3 * P, P, PACK - 1, banks[4:5])
-        deal(3, banks[4], PACK - 1, PACK)
+        weigh(3 * P, P, PACK - 1, banks[4:5])
+        deal(3, banks[4], PACK - 1, PACK, True)
         turn_back(3, banks[3])
+        quantize_out(0, 2 * P)
+        round_sbuf(2 * P, 3 * P)
+        quantize_out(2 * P, 3 * P)
         leave_f32(3, banks[3])
-        store_f32(3 * P, 4 * P)
+        store_f32(3 * P, 4 * P, nc.scalar)
         round_sbuf(3 * P, 4 * P)
         quantize_out(3 * P, 4 * P)
-
-        for r in range(4):
-            nc.sync.dma_start(out=out_2[0, r:16:4, :].bitcast(I32), in_=out_plane[r:P:32, :].bitcast(I32))
+        store_scales()

@@ -24,7 +24,7 @@ PASSES = K // (P * PACK)
 GROUPS = (3, 3, 3, 3)
 HALF = T // 2
 V_SHARE = 44
-RING = 6
+RING = 10
 
 
 def tile_moe_sup_lin_relu_kernel(
@@ -96,9 +96,9 @@ def tile_moe_sup_lin_relu_kernel(
         w1_codes = [keep.tile([P, H], U32, name="w1_codes%d" % s, align_bytes=64) for s in range(PASSES)]
         w1_plane = [keep.tile([P, H], U8, name="w1_plane%d" % s, align_bytes=64) for s in range(PASSES)]
 
-        def round_w1(on_vector, s, raw, raw_m0, m0, m1):
-            src = raw[:].rearrange("p j (m d) -> p m d j", d=PACK)[:, m0 - raw_m0 : m1 - raw_m0]
-            dst = w1_bf[s][:].rearrange("p d m j -> p m d j")[:, m0:m1]
+        def round_w1(on_vector, s, raw, raw_m0, m0, m1, d0=0, d1=PACK):
+            src = raw[:].rearrange("p j (m d) -> p m d j", d=PACK)[:, m0 - raw_m0 : m1 - raw_m0, d0:d1]
+            dst = w1_bf[s][:].rearrange("p d m j -> p m d j")[:, m0:m1, d0:d1]
             if on_vector:
                 nc.vector.tensor_copy(out=dst, in_=src)
             else:
@@ -116,10 +116,12 @@ def tile_moe_sup_lin_relu_kernel(
         round_w1(False, 0, w1_first, 0, 2 * V_SHARE, P)
         quantize_w1(0, 0)
         quantize_w1(0, 1)
-        for a in range(2):
-            round_w1(True, 1, w1_second[a], 64 * a, 64 * a, 64 * a + V_SHARE)
-            round_w1(False, 1, w1_second[a], 64 * a, 64 * a + V_SHARE, 64 * (a + 1))
+        round_w1(True, 1, w1_second[0], 0, 0, V_SHARE)
+        round_w1(False, 1, w1_second[0], 0, V_SHARE, 64)
+        round_w1(True, 1, w1_second[1], 64, 64, 64 + V_SHARE, 0, 2)
+        round_w1(False, 1, w1_second[1], 64, 64 + V_SHARE, P, 0, 2)
         quantize_w1(1, 0)
+        round_w1(False, 1, w1_second[1], 64, 64, P, 2, PACK)
         quantize_w1(1, 1)
 
         h_acc = [[banks[2 * u + th][:].rearrange("p (e t) -> p e t", e=2) for th in range(2)] for u in range(2)]
@@ -220,7 +222,7 @@ def tile_moe_sup_lin_relu_kernel(
         prods_made = []
 
         def on_scalar(j, r):
-            return j > 0 and r > 0
+            return (j > 0 and r == 2) or (j > 1 and r == 1)
 
         plains = {
             (j, r): keep.tile([P, T], F32, name="plain%d_%d" % (j, r))
@@ -291,18 +293,18 @@ def tile_moe_sup_lin_relu_kernel(
 
         def store_scales():
             for r in range(4):
-                nc.sync.dma_start(out=out_2[0, r:16:4, :].bitcast(I32), in_=out_plane[r:P:32, :].bitcast(I32))
+                queue = nc.sync if r < 2 else nc.scalar
+                queue.dma_start(out=out_2[0, r:16:4, :].bitcast(I32), in_=out_plane[r:P:32, :].bitcast(I32))
 
         fetch_plain(0, 2 * P)
         for j in range(PACK):
             weigh(0, 2 * P, j, banks[4:6])
-        fetch_plain(2 * P, P)
+        fetch_plain(2 * P, 2 * P)
         for b in range(2):
             deal(b, banks[4 + b], 0, PACK)
             turn_back(b, banks[b])
         for j in range(PACK):
             weigh(2 * P, P, j, banks[6:7])
-        fetch_plain(3 * P, P)
         for b in range(2):
             leave_f32(b, banks[b])
         store_f32(0, 2 * P)
@@ -317,12 +319,18 @@ def tile_moe_sup_lin_relu_kernel(
         deal(3, banks[7], 0, PACK - 1)
         weigh(3 * P, P, PACK - 1, banks[4:5])
         deal(3, banks[4], PACK - 1, PACK, True)
-        turn_back(3, banks[3])
-        quantize_out(0, 2 * P)
+        last_banks = (banks[3], banks[5])
+        for d in range(PACK):
+            nc.tensor.transpose(last_banks[d // 2][:, P * (d % 2) : P * (d % 2 + 1)], dealt[3][:, d, :], ident[:])
         round_sbuf(2 * P, 3 * P)
+        quantize_out(0, 2 * P)
         quantize_out(2 * P, 3 * P)
-        leave_f32(3, banks[3])
+        for u in range(2):
+            pair = last_banks[u][:, : 2 * P]
+            move(u == 1, out_bf[:, 3 * P :, 2 * u : 2 * u + 2], pair.rearrange("p (e t) -> p t e", e=2))
+        for u in range(2):
+            pair = last_banks[u][:, : 2 * P]
+            move(u == 1, out_f32[:, 2 * u : 2 * u + 2, 3 * P :], pair.rearrange("p (e t) -> p e t", e=2))
         store_f32(3 * P, 4 * P, nc.scalar)
-        round_sbuf(3 * P, 4 * P)
         quantize_out(3 * P, 4 * P)
         store_scales()

@@ -21,7 +21,13 @@ MULT = mybir.AluOpType.mult
 P = 128
 PACK = 4
 PASSES = K // (P * PACK)
-GROUPS = (3, 3, 3, 3)
+BANKS, BANK_COLS = 8, 512
+LIST_ROWS = 16
+QUAD = 32
+SCALE_ROWS = 16
+GROUP = 3
+GROUPS = E // GROUP
+GSLOTS = GROUP * C
 HALF = T // 2
 V_SHARE = 44
 RING = 10
@@ -31,18 +37,19 @@ def tile_moe_sup_lin_relu_kernel(
     tc, x_words, x_scales, w1, w2_words, w2_scales, gate, offs, pos1, pos2, pos3, out_0, out_1, out_2
 ):
     nc = tc.nc
-    first_expert = [sum(GROUPS[:g]) for g in range(len(GROUPS) + 1)]
-    last = len(GROUPS) - 1
     with ExitStack() as ctx:
         keep = ctx.enter_context(tc.tile_pool(name="keep", bufs=1))
         psum = ctx.enter_context(tc.psum_pool(name="psum", bufs=1))
-        banks = [psum.tile([P, 512], F32, name="bank%d" % i) for i in range(8)]
+        banks = [psum.tile([P, BANK_COLS], F32, name="bank%d" % i) for i in range(BANKS)]
 
         def move(on_vector, dst, src):
             if on_vector:
                 nc.vector.tensor_copy(out=dst, in_=src)
             else:
                 nc.scalar.copy(out=dst, in_=src)
+
+        def list_cols(first, count):
+            return slice(first // LIST_ROWS, (first + count) // LIST_ROWS)
 
         x_plane = keep.tile([P, PASSES, T], U8, name="x_plane", align_bytes=64)
         w2_plane = keep.tile([P, E, N], U8, name="w2_plane", align_bytes=64)
@@ -51,13 +58,13 @@ def tile_moe_sup_lin_relu_kernel(
         ident = keep.tile([P, P], F32, name="ident")
         make_identity(nc, ident[:])
 
-        w1_rows = w1.rearrange("(s p j) c -> s p j c", s=PASSES, j=PACK)
+        w1_rows = w1.rearrange("(s p a) c -> s p a c", s=PASSES, a=PACK)
         w1_first = keep.tile([P, PACK, H], F32, name="w1_first")
         nc.sync.dma_start(out=w1_first[:], in_=w1_rows[0])
-        for r in range(4):
+        for q in range(PACK):
             nc.sync.dma_start(
-                out=x_plane[r:P:32, :, :].bitcast(I32),
-                in_=x_scales[:, r:16:4, :].rearrange("s q t -> q s t").bitcast(I32),
+                out=x_plane[q:P:QUAD, :, :].bitcast(I32),
+                in_=x_scales[:, q:SCALE_ROWS:PACK, :].rearrange("s q t -> q s t").bitcast(I32),
             )
         x_codes = [keep.tile([P, T], U32, name="x_codes%d" % s, align_bytes=64) for s in range(PASSES)]
 
@@ -67,38 +74,47 @@ def tile_moe_sup_lin_relu_kernel(
             )
 
         load_x(0)
-        w1_second = [keep.tile([P, PACK, H // 2], F32, name="w1_second%d" % a) for a in range(2)]
-        for a in range(2):
-            nc.sync.dma_start(out=w1_second[a][:], in_=w1_rows[1][:, :, a * (H // 2) : (a + 1) * (H // 2)])
-        load_x(1)
-        offs_t = keep.tile([P, SLOTS // 16], U16, name="offs_t")
-        nc.sync.dma_start(offs_t[:], offs)
-        for r in range(4):
+        w1_second = [keep.tile([P, PACK, H // 2], F32, name="w1_second%d" % side) for side in range(2)]
+        for side in range(2):
             nc.sync.dma_start(
-                out=w2_plane[r:P:32, :, :].bitcast(I32),
-                in_=w2_scales[:, 0, r:16:4, :].rearrange("e q n -> q e n").bitcast(I32),
+                out=w1_second[side][:], in_=w1_rows[1][:, :, side * (H // 2) : (side + 1) * (H // 2)]
             )
-        w2_codes = [
-            keep.tile([P, size, 2 * N], U8, name="w2_codes%d" % g, align_bytes=64) for g, size in enumerate(GROUPS)
-        ]
-        for g in range(len(GROUPS)):
+        load_x(1)
+        offs_t = keep.tile([P, SLOTS // LIST_ROWS], U16, name="offs_t")
+        nc.sync.dma_start(offs_t[:], offs)
+        w2_codes = [keep.tile([P, GROUP, 2 * N], U8, name="w2_codes%d" % g, align_bytes=64) for g in range(GROUPS)]
+
+        def load_w2_scales(e0, e1):
+            for q in range(PACK):
+                nc.sync.dma_start(
+                    out=w2_plane[q:P:QUAD, e0:e1, :].bitcast(I32),
+                    in_=w2_scales[e0:e1, 0, q:SCALE_ROWS:PACK, :].rearrange("e q n -> q e n").bitcast(I32),
+                )
+
+        def load_w2_words(g):
             nc.sync.dma_start(
                 out=w2_codes[g][:].bitcast(I32),
-                in_=w2_words[first_expert[g] : first_expert[g + 1], 0].rearrange("e p b -> p e b").bitcast(I32),
+                in_=w2_words[GROUP * g : GROUP * (g + 1), 0].rearrange("e p c -> p e c").bitcast(I32),
             )
-        pos_t = [keep.tile([P, T // 16], U16, name="pos_t%d" % r) for r in range(TOP)]
+
+        pos_t = [keep.tile([P, T // LIST_ROWS], U16, name="pos_t%d" % r) for r in range(TOP)]
+        gate_t = keep.tile([P, TOP, T], F32, name="gate_t")
+        load_w2_scales(0, GROUP)
+        load_w2_words(0)
+        load_w2_scales(GROUP, E)
+        for g in range(1, GROUPS):
+            load_w2_words(g)
+        nc.sync.dma_start(out=gate_t[:], in_=gate.rearrange("r p t -> p r t"))
         for r, pos in enumerate((pos1, pos2, pos3)):
             nc.sync.dma_start(pos_t[r][:], pos)
-        gate_t = keep.tile([P, TOP, T], F32, name="gate_t")
-        nc.sync.dma_start(out=gate_t[:], in_=gate.rearrange("r p t -> p r t"))
 
         w1_bf = [keep.tile([P, PACK, P, PACK], BF16, name="w1_bf%d" % s, align_bytes=64) for s in range(PASSES)]
         w1_codes = [keep.tile([P, H], U32, name="w1_codes%d" % s, align_bytes=64) for s in range(PASSES)]
         w1_plane = [keep.tile([P, H], U8, name="w1_plane%d" % s, align_bytes=64) for s in range(PASSES)]
 
         def round_w1(on_vector, s, raw, raw_m0, m0, m1, d0=0, d1=PACK):
-            src = raw[:].rearrange("p j (m d) -> p m d j", d=PACK)[:, m0 - raw_m0 : m1 - raw_m0, d0:d1]
-            dst = w1_bf[s][:].rearrange("p d m j -> p m d j")[:, m0:m1, d0:d1]
+            src = raw[:].rearrange("p a (m d) -> p m d a", d=PACK)[:, m0 - raw_m0 : m1 - raw_m0, d0:d1]
+            dst = w1_bf[s][:].rearrange("p d m a -> p m d a")[:, m0:m1, d0:d1]
             if on_vector:
                 nc.vector.tensor_copy(out=dst, in_=src)
             else:
@@ -109,43 +125,44 @@ def tile_moe_sup_lin_relu_kernel(
             nc.vector.quantize_mx(
                 out=w1_codes[s][:, cols].bitcast(FP8X4),
                 scales=w1_plane[s][:, cols],
-                in_=w1_bf[s][:, 2 * u : 2 * u + 2].rearrange("p d m j -> p (d m j)"),
+                in_=w1_bf[s][:, 2 * u : 2 * u + 2].rearrange("p d m a -> p (d m a)"),
             )
 
+        mid = P // 2
         round_w1(True, 0, w1_first, 0, 0, 2 * V_SHARE)
         round_w1(False, 0, w1_first, 0, 2 * V_SHARE, P)
         quantize_w1(0, 0)
         quantize_w1(0, 1)
         round_w1(True, 1, w1_second[0], 0, 0, V_SHARE)
-        round_w1(False, 1, w1_second[0], 0, V_SHARE, 64)
-        round_w1(True, 1, w1_second[1], 64, 64, 64 + V_SHARE, 0, 2)
-        round_w1(False, 1, w1_second[1], 64, 64 + V_SHARE, P, 0, 2)
+        round_w1(False, 1, w1_second[0], 0, V_SHARE, mid)
+        round_w1(True, 1, w1_second[1], mid, mid, mid + V_SHARE, 0, 2)
+        round_w1(False, 1, w1_second[1], mid, mid + V_SHARE, P, 0, 2)
         quantize_w1(1, 0)
-        round_w1(False, 1, w1_second[1], 64, 64, P, 2, PACK)
+        round_w1(False, 1, w1_second[1], mid, mid, P, 2, PACK)
         quantize_w1(1, 1)
 
-        h_acc = [[banks[2 * u + th][:].rearrange("p (e t) -> p e t", e=2) for th in range(2)] for u in range(2)]
+        h_acc = [[banks[2 * u + side][:].rearrange("p (e t) -> p e t", e=2) for side in range(2)] for u in range(2)]
         for s in range(PASSES):
             for u in range(2):
-                for th in range(2):
+                for side in range(2):
                     for e in range(2):
                         d = 2 * u + e
                         nc.tensor.matmul_mx(
-                            out=h_acc[u][th][:, e, :],
+                            out=h_acc[u][side][:, e, :],
                             lhsT=w1_codes[s][:, P * d : P * (d + 1)].bitcast(FP8X4),
                             lhsT_scale=w1_plane[s][:, P * d : P * (d + 1)],
-                            rhs=x_codes[s][:, HALF * th : HALF * (th + 1)].bitcast(FP8X4),
-                            rhs_scale=x_plane[:, s, HALF * th : HALF * (th + 1)],
+                            rhs=x_codes[s][:, HALF * side : HALF * (side + 1)].bitcast(FP8X4),
+                            rhs_scale=x_plane[:, s, HALF * side : HALF * (side + 1)],
                             start=(s == 0 and e == 0),
                             stop=(s == PASSES - 1 and e == 1),
                         )
         h_pairs = keep.tile([P, 2 * T], U32, name="h_pairs")
         for u in range(2):
-            for th in range(2):
-                first = T * u + HALF * th
+            for side in range(2):
+                first = T * u + HALF * side
                 dst = h_pairs[:, first : first + HALF].bitcast(BF16).rearrange("p (t e) -> p t e", e=2)
-                src = h_acc[u][th].rearrange("p e t -> p t e")
-                if u == 0 and th == 1:
+                src = h_acc[u][side].rearrange("p e t -> p t e")
+                if u == 0 and side == 1:
                     nc.vector.tensor_scalar_max(dst, src, 0.0)
                 else:
                     nc.scalar.activation(dst, src, ACT.Relu)
@@ -153,19 +170,20 @@ def tile_moe_sup_lin_relu_kernel(
         slot_codes = keep.tile([P, SLOTS], U32, name="slot_codes", align_bytes=64)
         slot_plane = keep.tile([P, SLOTS], U8, name="slot_plane", align_bytes=64)
         y_rows = [keep.tile([P, SLOTS], F32, name="y_rows%d" % j) for j in range(PACK)]
-        stage = [keep.tile([P, 2 * C * max(GROUPS)], U32, name="stage%d" % i, align_bytes=64) for i in range(3)]
+        stage = keep.tile([P, 6 * GSLOTS], U32, name="stage", align_bytes=64)
+        picked_at = (0, 4, 2, 1)
+        woven_at = (2, 0, 4, 4)
+        last = GROUPS - 1
 
-        def pick(g):
-            width = C * GROUPS[g]
-            cols = slice(C * first_expert[g] // 16, C * first_expert[g + 1] // 16)
-            for u in range(2):
+        def pick(g, halves=(0, 1)):
+            for u in halves:
                 window = h_pairs[:] if (g > 0 and u == 0) else h_pairs[:, T * u : T * (u + 1)]
-                dst = stage[2 * g % 3][:, width * u : width * (u + 1)]
-                nc.vector.tensor_copy(out=dst, in_=window.indirect(offs_t[:, cols]))
+                dst = stage[:, GSLOTS * (picked_at[g] + u) : GSLOTS * (picked_at[g] + u + 1)]
+                nc.vector.tensor_copy(out=dst, in_=window.indirect(offs_t[:, list_cols(GSLOTS * g, GSLOTS)]))
 
         def weave_and_quantize(g):
-            width = C * GROUPS[g]
-            picked, woven = stage[2 * g % 3][:, : 2 * width], stage[(2 * g + 1) % 3][:, : 2 * width]
+            picked = stage[:, GSLOTS * picked_at[g] : GSLOTS * (picked_at[g] + 2)]
+            woven = stage[:, GSLOTS * woven_at[g] : GSLOTS * (woven_at[g] + 2)]
             if g == last:
                 nc.vector.tensor_copy(
                     out=woven.bitcast(I32).rearrange("p (s u) -> p s u", u=2),
@@ -175,18 +193,15 @@ def tile_moe_sup_lin_relu_kernel(
                 nc.scalar.copy(
                     out=woven.rearrange("p (s u) -> p s u", u=2), in_=picked.rearrange("p (u s) -> p s u", u=2)
                 )
-            slots = slice(C * first_expert[g], C * first_expert[g + 1])
+            slots = slice(GSLOTS * g, GSLOTS * (g + 1))
             nc.vector.quantize_mx(
                 out=slot_codes[:, slots].bitcast(FP8X4), scales=slot_plane[:, slots], in_=woven.bitcast(BF16)
             )
 
-        y_made = []
-
         def experts(g, j, on_vector=False):
-            y_acc = banks[(4 + len(y_made)) % 8]
-            y_made.append((g, j))
-            for i in range(GROUPS[g]):
-                e = first_expert[g] + i
+            y_acc = banks[(PACK + PACK * g + j) % BANKS]
+            for i in range(GROUP):
+                e = GROUP * g + i
                 nc.tensor.matmul_mx(
                     out=y_acc[:, C * i : C * (i + 1)],
                     lhsT=w2_codes[g][:, i, 2 * P * j : 2 * P * (j + 1)].bitcast(FP4X4),
@@ -196,24 +211,19 @@ def tile_moe_sup_lin_relu_kernel(
                     start=True,
                     stop=True,
                 )
-            move(on_vector, y_rows[j][:, C * first_expert[g] : C * first_expert[g + 1]], y_acc[:, : C * GROUPS[g]])
+            move(on_vector, y_rows[j][:, GSLOTS * g : GSLOTS * (g + 1)], y_acc[:, :GSLOTS])
 
-        for g in range(len(GROUPS)):
-            pick(g)
-            if 2 <= g < last:
+        for g in range(GROUPS):
+            pick(g, (1,) if g == last else (0, 1))
+            if g == last - 1:
+                pick(last, (0,))
                 for j in range(PACK - 1):
-                    experts(g - 2, j)
+                    experts(0, j)
             weave_and_quantize(g)
-            if 3 <= g < last:
-                experts(g - 3, PACK - 1)
-        if last >= 3:
-            experts(last - 3, PACK - 1)
-        for j in range(PACK):
-            experts(last - 2, j)
-        for j in range(PACK):
-            experts(last - 1, j, j == PACK - 1)
-        for j in range(PACK):
-            experts(last, j, j == 0)
+        experts(0, PACK - 1)
+        for g in range(1, GROUPS):
+            for j in range(PACK):
+                experts(g, j, (g, j) in ((last - 1, PACK - 1), (last, 0)))
 
         out_rows = out_0.rearrange("(m d) t -> m d t", d=PACK)
         out_words = out_1[0].rearrange("p t d -> p (t d)").bitcast(I32)
@@ -221,32 +231,31 @@ def tile_moe_sup_lin_relu_kernel(
         prods = [keep.tile([P, HALF], F32, name="prod%d" % i) for i in range(RING)]
         prods_made = []
 
-        def on_scalar(j, r):
-            return (j > 0 and r == 2) or (j > 1 and r == 1)
+        def on_scalar(j, r, t0):
+            return j > 0 and r > 0 and (t0 < HALF or (j, r) != (1, 1))
 
         plains = {
             (j, r): keep.tile([P, T], F32, name="plain%d_%d" % (j, r))
             for j in range(PACK)
             for r in range(TOP)
-            if on_scalar(j, r)
+            if on_scalar(j, r, 0)
         }
 
-        def fetch_plain(t0, width):
-            cols = slice(t0 // 16, (t0 + width) // 16)
+        def fetch_plain(t0):
             for j, r in plains:
-                nc.scalar.activation(
-                    plains[j, r][:, t0 : t0 + width], y_rows[j][:].indirect(pos_t[r][:, cols]), ACT.Copy
-                )
+                if on_scalar(j, r, t0):
+                    window = y_rows[j][:].indirect(pos_t[r][:, list_cols(t0, HALF)])
+                    nc.scalar.activation(plains[j, r][:, t0 : t0 + HALF], window, ACT.Copy)
 
-        def weigh(t0, width, j, sum_banks):
-            cols = slice(t0 // 16, (t0 + width) // 16)
+        def weigh(t0, j, sum_banks):
+            width = P * len(sum_banks)
             for r in range(TOP):
                 prod = prods[len(prods_made) % RING]
-                prods_made.append(r)
-                if on_scalar(j, r):
+                prods_made.append((t0, j, r))
+                if on_scalar(j, r, t0):
                     values = plains[j, r][:, t0 : t0 + width]
                 else:
-                    values = y_rows[j][:].indirect(pos_t[r][:, cols])
+                    values = y_rows[j][:].indirect(pos_t[r][:, list_cols(t0, width)])
                 nc.vector.tensor_tensor(prod[:, :width], values, gate_t[:, r, t0 : t0 + width], MULT)
                 for b, bank in enumerate(sum_banks):
                     nc.tensor.matmul(
@@ -258,14 +267,15 @@ def tile_moe_sup_lin_relu_kernel(
                         is_transpose=True,
                     )
 
-        dealt = [keep.tile([P, PACK, P], F32, name="dealt%d" % b) for b in range(4)]
+        dealt = [keep.tile([P, PACK, P], F32, name="dealt%d" % b) for b in range(T // P)]
         out_f32 = keep.tile([P, PACK, T], F32, name="out_f32")
         out_bf = keep.tile([P, T, PACK], BF16, name="out_bf", align_bytes=64)
         out_codes = keep.tile([P, T], U32, name="out_codes", align_bytes=64)
+        m_per_tile = P // PACK
 
-        def deal(b, bank, j0, j1, on_vector=False):
+        def deal(b, bank, j0=0, j1=PACK):
             src = bank[:, P * j0 : P * j1].rearrange("p (m d) -> p d m", d=PACK)
-            move(on_vector, dealt[b][:, :, 32 * j0 : 32 * j1], src)
+            nc.scalar.copy(out=dealt[b][:, :, m_per_tile * j0 : m_per_tile * j1], in_=src)
 
         def turn_back(b, bank):
             for d in range(PACK):
@@ -274,14 +284,11 @@ def tile_moe_sup_lin_relu_kernel(
         def leave_f32(b, bank):
             nc.scalar.copy(out=out_f32[:, :, P * b : P * (b + 1)], in_=bank[:].rearrange("p (d t) -> p d t", d=PACK))
 
-        def round_sbuf(t0, t1):
+        def store_f32(t0, t1):
+            nc.sync.dma_start(out=out_rows[:, :, t0:t1], in_=out_f32[:, :, t0:t1])
+
+        def round_out(t0, t1):
             nc.vector.tensor_copy(out=out_bf[:, t0:t1, :], in_=out_f32[:, :, t0:t1].rearrange("p d t -> p t d"))
-
-        def round_out(b, bank, on_vector=False):
-            move(on_vector, out_bf[:, P * b : P * (b + 1), :], bank[:].rearrange("p (d t) -> p t d", d=PACK))
-
-        def store_f32(t0, t1, queue=nc.sync):
-            queue.dma_start(out=out_rows[:, :, t0:t1], in_=out_f32[:, :, t0:t1])
 
         def quantize_out(t0, t1):
             nc.vector.quantize_mx(
@@ -291,46 +298,45 @@ def tile_moe_sup_lin_relu_kernel(
             )
             nc.sync.dma_start(out=out_words[:, t0:t1], in_=out_codes[:, t0:t1].bitcast(I32))
 
-        def store_scales():
-            for r in range(4):
-                queue = nc.sync if r < 2 else nc.scalar
-                queue.dma_start(out=out_2[0, r:16:4, :].bitcast(I32), in_=out_plane[r:P:32, :].bitcast(I32))
-
-        fetch_plain(0, 2 * P)
+        fetch_plain(0)
         for j in range(PACK):
-            weigh(0, 2 * P, j, banks[4:6])
-        fetch_plain(2 * P, 2 * P)
+            weigh(0, j, banks[4:6])
+        fetch_plain(HALF)
         for b in range(2):
-            deal(b, banks[4 + b], 0, PACK)
+            deal(b, banks[4 + b])
             turn_back(b, banks[b])
         for j in range(PACK):
-            weigh(2 * P, P, j, banks[6:7])
+            weigh(2 * P, j, banks[6:7])
         for b in range(2):
             leave_f32(b, banks[b])
         store_f32(0, 2 * P)
-        deal(2, banks[6], 0, PACK)
+        deal(2, banks[6])
         turn_back(2, banks[2])
-        for b in range(2):
-            round_out(b, banks[b])
         for j in range(PACK - 1):
-            weigh(3 * P, P, j, banks[7:8])
+            weigh(3 * P, j, banks[7:8])
         leave_f32(2, banks[2])
         store_f32(2 * P, 3 * P)
         deal(3, banks[7], 0, PACK - 1)
-        weigh(3 * P, P, PACK - 1, banks[4:5])
-        deal(3, banks[4], PACK - 1, PACK, True)
-        last_banks = (banks[3], banks[5])
+        weigh(3 * P, PACK - 1, banks[4:5])
+        deal(3, banks[4], PACK - 1, PACK)
+        pair_banks = (banks[3], banks[5])
         for d in range(PACK):
-            nc.tensor.transpose(last_banks[d // 2][:, P * (d % 2) : P * (d % 2 + 1)], dealt[3][:, d, :], ident[:])
-        round_sbuf(2 * P, 3 * P)
-        quantize_out(0, 2 * P)
-        quantize_out(2 * P, 3 * P)
+            nc.tensor.transpose(pair_banks[d // 2][:, P * (d % 2) : P * (d % 2 + 1)], dealt[3][:, d, :], ident[:])
+        round_out(0, 2 * P)
+        round_out(2 * P, 3 * P)
+        quantize_out(0, 3 * P)
         for u in range(2):
-            pair = last_banks[u][:, : 2 * P]
+            pair = pair_banks[u][:, : 2 * P]
             move(u == 1, out_bf[:, 3 * P :, 2 * u : 2 * u + 2], pair.rearrange("p (e t) -> p t e", e=2))
         for u in range(2):
-            pair = last_banks[u][:, : 2 * P]
+            pair = pair_banks[u][:, : 2 * P]
             move(u == 1, out_f32[:, 2 * u : 2 * u + 2, 3 * P :], pair.rearrange("p (e t) -> p e t", e=2))
-        store_f32(3 * P, 4 * P, nc.scalar)
-        quantize_out(3 * P, 4 * P)
-        store_scales()
+            nc.scalar.dma_start(
+                out=out_rows[:, 2 * u : 2 * u + 2, 3 * P :], in_=out_f32[:, 2 * u : 2 * u + 2, 3 * P :]
+            )
+        quantize_out(3 * P, T)
+        for q in range(PACK):
+            queue = nc.sync if q < PACK // 2 else nc.scalar
+            queue.dma_start(
+                out=out_2[0, q:SCALE_ROWS:PACK, :].bitcast(I32), in_=out_plane[q:P:QUAD, :].bitcast(I32)
+            )

from contextlib import ExitStack

import concourse.mybir as mybir
from concourse.masks import make_identity

K, T, E, C, H, N, TOP = 1024, 512, 12, 128, 512, 512, 3
SLOTS = E * C
FLOPS = 2 * K * H * T + 2 * H * N * SLOTS

F32 = mybir.dt.float32
BF16 = mybir.dt.bfloat16
I32 = mybir.dt.int32
U32 = mybir.dt.uint32
U16 = mybir.dt.uint16
U8 = mybir.dt.uint8
FP8X4 = mybir.dt.float8_e4m3fn_x4
FP4X4 = mybir.dt.float4_e2m1fn_x4
ACT = mybir.ActivationFunctionType
MULT = mybir.AluOpType.mult

P = 128
PACK = 4
PASSES = K // (P * PACK)
BANKS, BANK_COLS = 8, 512
LIST_ROWS = 16
QUAD = 32
SCALE_ROWS = 16
GROUP = 3
GROUPS = E // GROUP
GSLOTS = GROUP * C
HALF = T // 2
V_SHARE = 44
RING = 10


def tile_moe_sup_lin_relu_kernel(
    tc, x_words, x_scales, w1, w2_words, w2_scales, gate, offs, pos1, pos2, pos3, out_0, out_1, out_2
):
    nc = tc.nc
    with ExitStack() as ctx:
        keep = ctx.enter_context(tc.tile_pool(name="keep", bufs=1))
        psum = ctx.enter_context(tc.psum_pool(name="psum", bufs=1))
        banks = [psum.tile([P, BANK_COLS], F32, name="bank%d" % i) for i in range(BANKS)]

        def move(on_vector, dst, src):
            if on_vector:
                nc.vector.tensor_copy(out=dst, in_=src)
            else:
                nc.scalar.copy(out=dst, in_=src)

        def list_cols(first, count):
            return slice(first // LIST_ROWS, (first + count) // LIST_ROWS)

        x_plane = keep.tile([P, PASSES, T], U8, name="x_plane", align_bytes=64)
        w2_plane = keep.tile([P, E, N], U8, name="w2_plane", align_bytes=64)
        nc.vector.memset(x_plane[:].rearrange("p s t -> p (s t)").bitcast(I32), 0)
        nc.vector.memset(w2_plane[:].rearrange("p e n -> p (e n)").bitcast(I32), 0)
        ident = keep.tile([P, P], F32, name="ident")
        make_identity(nc, ident[:])

        w1_rows = w1.rearrange("(s p a) c -> s p a c", s=PASSES, a=PACK)
        w1_first = keep.tile([P, PACK, H], F32, name="w1_first")
        nc.sync.dma_start(out=w1_first[:], in_=w1_rows[0])
        for q in range(PACK):
            nc.sync.dma_start(
                out=x_plane[q:P:QUAD, :, :].bitcast(I32),
                in_=x_scales[:, q:SCALE_ROWS:PACK, :].rearrange("s q t -> q s t").bitcast(I32),
            )
        x_codes = [keep.tile([P, T], U32, name="x_codes%d" % s, align_bytes=64) for s in range(PASSES)]

        def load_x(s):
            nc.sync.dma_start(
                out=x_codes[s][:].bitcast(I32), in_=x_words[s].rearrange("p t d -> p (t d)").bitcast(I32)
            )

        load_x(0)
        w1_second = [keep.tile([P, PACK, H // 2], F32, name="w1_second%d" % side) for side in range(2)]
        for side in range(2):
            nc.sync.dma_start(
                out=w1_second[side][:], in_=w1_rows[1][:, :, side * (H // 2) : (side + 1) * (H // 2)]
            )
        load_x(1)
        offs_t = keep.tile([P, SLOTS // LIST_ROWS], U16, name="offs_t")
        nc.sync.dma_start(offs_t[:], offs)
        w2_codes = [keep.tile([P, GROUP, 2 * N], U8, name="w2_codes%d" % g, align_bytes=64) for g in range(GROUPS)]

        def load_w2_scales(e0, e1):
            for q in range(PACK):
                nc.sync.dma_start(
                    out=w2_plane[q:P:QUAD, e0:e1, :].bitcast(I32),
                    in_=w2_scales[e0:e1, 0, q:SCALE_ROWS:PACK, :].rearrange("e q n -> q e n").bitcast(I32),
                )

        def load_w2_words(g):
            nc.sync.dma_start(
                out=w2_codes[g][:].bitcast(I32),
                in_=w2_words[GROUP * g : GROUP * (g + 1), 0].rearrange("e p c -> p e c").bitcast(I32),
            )

        pos_t = [keep.tile([P, T // LIST_ROWS], U16, name="pos_t%d" % r) for r in range(TOP)]
        gate_t = keep.tile([P, TOP, T], F32, name="gate_t")
        load_w2_scales(0, GROUP)
        load_w2_words(0)
        load_w2_scales(GROUP, E)
        for g in range(1, GROUPS):
            load_w2_words(g)
        nc.sync.dma_start(out=gate_t[:], in_=gate.rearrange("r p t -> p r t"))
        for r, pos in enumerate((pos1, pos2, pos3)):
            nc.sync.dma_start(pos_t[r][:], pos)

        w1_bf = [keep.tile([P, PACK, P, PACK], BF16, name="w1_bf%d" % s, align_bytes=64) for s in range(PASSES)]
        w1_codes = [keep.tile([P, H], U32, name="w1_codes%d" % s, align_bytes=64) for s in range(PASSES)]
        w1_plane = [keep.tile([P, H], U8, name="w1_plane%d" % s, align_bytes=64) for s in range(PASSES)]

        def round_w1(on_vector, s, raw, raw_m0, m0, m1, d0=0, d1=PACK):
            src = raw[:].rearrange("p a (m d) -> p m d a", d=PACK)[:, m0 - raw_m0 : m1 - raw_m0, d0:d1]
            dst = w1_bf[s][:].rearrange("p d m a -> p m d a")[:, m0:m1, d0:d1]
            if on_vector:
                nc.vector.tensor_copy(out=dst, in_=src)
            else:
                nc.scalar.activation(dst, src, ACT.Copy)

        def quantize_w1(s, u):
            cols = slice(2 * P * u, 2 * P * (u + 1))
            nc.vector.quantize_mx(
                out=w1_codes[s][:, cols].bitcast(FP8X4),
                scales=w1_plane[s][:, cols],
                in_=w1_bf[s][:, 2 * u : 2 * u + 2].rearrange("p d m a -> p (d m a)"),
            )

        mid = P // 2
        round_w1(True, 0, w1_first, 0, 0, 2 * V_SHARE)
        round_w1(False, 0, w1_first, 0, 2 * V_SHARE, P)
        quantize_w1(0, 0)
        quantize_w1(0, 1)
        round_w1(True, 1, w1_second[0], 0, 0, V_SHARE)
        round_w1(False, 1, w1_second[0], 0, V_SHARE, mid)
        round_w1(True, 1, w1_second[1], mid, mid, mid + V_SHARE, 0, 2)
        round_w1(False, 1, w1_second[1], mid, mid + V_SHARE, P, 0, 2)
        quantize_w1(1, 0)
        round_w1(False, 1, w1_second[1], mid, mid, P, 2, PACK)
        quantize_w1(1, 1)

        h_acc = [[banks[2 * u + side][:].rearrange("p (e t) -> p e t", e=2) for side in range(2)] for u in range(2)]
        for s in range(PASSES):
            for u in range(2):
                for side in range(2):
                    for e in range(2):
                        d = 2 * u + e
                        nc.tensor.matmul_mx(
                            out=h_acc[u][side][:, e, :],
                            lhsT=w1_codes[s][:, P * d : P * (d + 1)].bitcast(FP8X4),
                            lhsT_scale=w1_plane[s][:, P * d : P * (d + 1)],
                            rhs=x_codes[s][:, HALF * side : HALF * (side + 1)].bitcast(FP8X4),
                            rhs_scale=x_plane[:, s, HALF * side : HALF * (side + 1)],
                            start=(s == 0 and e == 0),
                            stop=(s == PASSES - 1 and e == 1),
                        )
        h_pairs = keep.tile([P, 2 * T], U32, name="h_pairs")
        for u in range(2):
            for side in range(2):
                first = T * u + HALF * side
                dst = h_pairs[:, first : first + HALF].bitcast(BF16).rearrange("p (t e) -> p t e", e=2)
                src = h_acc[u][side].rearrange("p e t -> p t e")
                if u == 0 and side == 1:
                    nc.vector.tensor_scalar_max(dst, src, 0.0)
                else:
                    nc.scalar.activation(dst, src, ACT.Relu)

        slot_codes = keep.tile([P, SLOTS], U32, name="slot_codes", align_bytes=64)
        slot_plane = keep.tile([P, SLOTS], U8, name="slot_plane", align_bytes=64)
        y_rows = [keep.tile([P, SLOTS], F32, name="y_rows%d" % j) for j in range(PACK)]
        stage = keep.tile([P, 6 * GSLOTS], U32, name="stage", align_bytes=64)
        picked_at = (0, 4, 2, 1)
        woven_at = (2, 0, 4, 4)
        last = GROUPS - 1

        def pick(g, halves=(0, 1)):
            for u in halves:
                window = h_pairs[:] if (g > 0 and u == 0) else h_pairs[:, T * u : T * (u + 1)]
                dst = stage[:, GSLOTS * (picked_at[g] + u) : GSLOTS * (picked_at[g] + u + 1)]
                nc.vector.tensor_copy(out=dst, in_=window.indirect(offs_t[:, list_cols(GSLOTS * g, GSLOTS)]))

        def weave_and_quantize(g):
            picked = stage[:, GSLOTS * picked_at[g] : GSLOTS * (picked_at[g] + 2)]
            woven = stage[:, GSLOTS * woven_at[g] : GSLOTS * (woven_at[g] + 2)]
            if g == last:
                nc.vector.tensor_copy(
                    out=woven.bitcast(I32).rearrange("p (s u) -> p s u", u=2),
                    in_=picked.bitcast(I32).rearrange("p (u s) -> p s u", u=2),
                )
            else:
                nc.scalar.copy(
                    out=woven.rearrange("p (s u) -> p s u", u=2), in_=picked.rearrange("p (u s) -> p s u", u=2)
                )
            slots = slice(GSLOTS * g, GSLOTS * (g + 1))
            nc.vector.quantize_mx(
                out=slot_codes[:, slots].bitcast(FP8X4), scales=slot_plane[:, slots], in_=woven.bitcast(BF16)
            )

        def experts(g, j, on_vector=False):
            y_acc = banks[(PACK + PACK * g + j) % BANKS]
            for i in range(GROUP):
                e = GROUP * g + i
                nc.tensor.matmul_mx(
                    out=y_acc[:, C * i : C * (i + 1)],
                    lhsT=w2_codes[g][:, i, 2 * P * j : 2 * P * (j + 1)].bitcast(FP4X4),
                    lhsT_scale=w2_plane[:, e, P * j : P * (j + 1)],
                    rhs=slot_codes[:, C * e : C * (e + 1)].bitcast(FP8X4),
                    rhs_scale=slot_plane[:, C * e : C * (e + 1)],
                    start=True,
                    stop=True,
                )
            move(on_vector, y_rows[j][:, GSLOTS * g : GSLOTS * (g + 1)], y_acc[:, :GSLOTS])

        for g in range(GROUPS):
            pick(g, (1,) if g == last else (0, 1))
            if g == last - 1:
                pick(last, (0,))
                for j in range(PACK - 1):
                    experts(0, j)
            weave_and_quantize(g)
        experts(0, PACK - 1)
        for g in range(1, GROUPS):
            for j in range(PACK):
                experts(g, j, (g, j) in ((last - 1, PACK - 1), (last, 0)))

        out_rows = out_0.rearrange("(m d) t -> m d t", d=PACK)
        out_words = out_1[0].rearrange("p t d -> p (t d)").bitcast(I32)
        out_plane = keep.tile([P, T], U8, name="out_plane", align_bytes=64)
        prods = [keep.tile([P, HALF], F32, name="prod%d" % i) for i in range(RING)]
        prods_made = []

        def on_scalar(j, r, t0):
            return j > 0 and r > 0 and (t0 < HALF or (j, r) != (1, 1))

        plains = {
            (j, r): keep.tile([P, T], F32, name="plain%d_%d" % (j, r))
            for j in range(PACK)
            for r in range(TOP)
            if on_scalar(j, r, 0)
        }

        def fetch_plain(t0):
            for j, r in plains:
                if on_scalar(j, r, t0):
                    window = y_rows[j][:].indirect(pos_t[r][:, list_cols(t0, HALF)])
                    nc.scalar.activation(plains[j, r][:, t0 : t0 + HALF], window, ACT.Copy)

        def weigh(t0, j, sum_banks):
            width = P * len(sum_banks)
            for r in range(TOP):
                prod = prods[len(prods_made) % RING]
                prods_made.append((t0, j, r))
                if on_scalar(j, r, t0):
                    values = plains[j, r][:, t0 : t0 + width]
                else:
                    values = y_rows[j][:].indirect(pos_t[r][:, list_cols(t0, width)])
                nc.vector.tensor_tensor(prod[:, :width], values, gate_t[:, r, t0 : t0 + width], MULT)
                for b, bank in enumerate(sum_banks):
                    nc.tensor.matmul(
                        bank[:, P * j : P * (j + 1)],
                        prod[:, P * b : P * (b + 1)],
                        ident[:],
                        start=(r == 0),
                        stop=(r == TOP - 1),
                        is_transpose=True,
                    )

        dealt = [keep.tile([P, PACK, P], F32, name="dealt%d" % b) for b in range(T // P)]
        out_f32 = keep.tile([P, PACK, T], F32, name="out_f32")
        out_bf = keep.tile([P, T, PACK], BF16, name="out_bf", align_bytes=64)
        out_codes = keep.tile([P, T], U32, name="out_codes", align_bytes=64)
        m_per_tile = P // PACK

        def deal(b, bank, j0=0, j1=PACK):
            src = bank[:, P * j0 : P * j1].rearrange("p (m d) -> p d m", d=PACK)
            nc.scalar.copy(out=dealt[b][:, :, m_per_tile * j0 : m_per_tile * j1], in_=src)

        def turn_back(b, bank):
            for d in range(PACK):
                nc.tensor.transpose(bank[:, P * d : P * (d + 1)], dealt[b][:, d, :], ident[:])

        def leave_f32(b, bank):
            nc.scalar.copy(out=out_f32[:, :, P * b : P * (b + 1)], in_=bank[:].rearrange("p (d t) -> p d t", d=PACK))

        def store_f32(t0, t1):
            nc.sync.dma_start(out=out_rows[:, :, t0:t1], in_=out_f32[:, :, t0:t1])

        def round_out(t0, t1):
            nc.vector.tensor_copy(out=out_bf[:, t0:t1, :], in_=out_f32[:, :, t0:t1].rearrange("p d t -> p t d"))

        def quantize_out(t0, t1):
            nc.vector.quantize_mx(
                out=out_codes[:, t0:t1].bitcast(FP8X4),
                scales=out_plane[:, t0:t1],
                in_=out_bf[:, t0:t1, :].rearrange("p t d -> p (t d)"),
            )
            nc.sync.dma_start(out=out_words[:, t0:t1], in_=out_codes[:, t0:t1].bitcast(I32))

        fetch_plain(0)
        for j in range(PACK):
            weigh(0, j, banks[4:6])
        fetch_plain(HALF)
        for b in range(2):
            deal(b, banks[4 + b])
            turn_back(b, banks[b])
        for j in range(PACK):
            weigh(2 * P, j, banks[6:7])
        for b in range(2):
            leave_f32(b, banks[b])
        store_f32(0, 2 * P)
        deal(2, banks[6])
        turn_back(2, banks[2])
        for j in range(PACK - 1):
            weigh(3 * P, j, banks[7:8])
        leave_f32(2, banks[2])
        store_f32(2 * P, 3 * P)
        deal(3, banks[7], 0, PACK - 1)
        weigh(3 * P, PACK - 1, banks[4:5])
        deal(3, banks[4], PACK - 1, PACK)
        pair_banks = (banks[3], banks[5])
        for d in range(PACK):
            nc.tensor.transpose(pair_banks[d // 2][:, P * (d % 2) : P * (d % 2 + 1)], dealt[3][:, d, :], ident[:])
        round_out(0, 2 * P)
        round_out(2 * P, 3 * P)
        quantize_out(0, 3 * P)
        for u in range(2):
            pair = pair_banks[u][:, : 2 * P]
            move(u == 1, out_bf[:, 3 * P :, 2 * u : 2 * u + 2], pair.rearrange("p (e t) -> p t e", e=2))
        for u in range(2):
            pair = pair_banks[u][:, : 2 * P]
            move(u == 1, out_f32[:, 2 * u : 2 * u + 2, 3 * P :], pair.rearrange("p (e t) -> p e t", e=2))
            nc.scalar.dma_start(
                out=out_rows[:, 2 * u : 2 * u + 2, 3 * P :], in_=out_f32[:, 2 * u : 2 * u + 2, 3 * P :]
            )
        quantize_out(3 * P, T)
        for q in range(PACK):
            queue = nc.sync if q < PACK // 2 else nc.scalar
            queue.dma_start(
                out=out_2[0, q:SCALE_ROWS:PACK, :].bitcast(I32), in_=out_plane[q:P:QUAD, :].bitcast(I32)
            )
